import numpy as np, ml_dtypes
CORES = [51,54,179,182]
N = 4
KB, QP = 1, 128
def setup_inputs(rng):
    q = rng.standard_normal((N, 128, QP), dtype=np.float32) / 4; k = rng.standard_normal((N, 128, KB * 128), dtype=np.float32)
    a = 2 * np.pi * rng.random((N, QP)); s = 400 * rng.random((N, QP)) ** 1.5; q[:, 0, :] = s * np.cos(a); q[:, 1, :] = s * np.sin(a); q[:, 2, :] = 150 * rng.standard_normal((N, QP)); k[:, 2, :] = 1 + k[:, 2, :] / 50
    a = (2 * np.pi * rng.random() + np.pi / 2 * (rng.permutation(N).reshape(N, 1, 1) + 0.5) / N - 0.5 + (np.arange(KB).reshape(1, KB, 1) + rng.random((N, KB, 128))) / KB).reshape(N, KB * 128); k[:, 0, :] = np.cos(a); k[:, 1, :] = np.sin(a)
    return {"q": q.astype(ml_dtypes.bfloat16), "k": k.astype(ml_dtypes.bfloat16), "v": rng.standard_normal((N, 128, KB * 128), dtype=np.float32).astype(ml_dtypes.bfloat16)}
def setup_inputs_big(rng):
    d = setup_inputs(rng)
    for k in ("v",): d[k] = (d[k].astype(np.float32) * 1048576.0).astype(d[k].dtype)
    return d
def setup_inputs_small(rng):
    d = setup_inputs(rng)
    for k in ("v",): d[k] = (d[k].astype(np.float32) * (1 / 1048576.0)).astype(d[k].dtype)
    return d
def reference(q, k, v):
    Q, K, V = q.astype(np.float64), k.astype(np.float64), v.astype(np.float64)
    y = np.zeros((N, QP, 128))
    for r in range(N):
        js = list(range(N))
        S = np.concatenate([K[j].T @ Q[r] for j in js], axis=0)
        P = np.exp(S - S.max(axis=0)); P = P / P.sum(axis=0)
        y[r] = P.T @ np.concatenate([V[j][:, 128 * b:128 * b + 128] for j in js for b in range(KB)], axis=0)
    return {"y": y.astype(ml_dtypes.bfloat16)}

@@ -1,0 +1,183 @@
+from concourse.bass import DstId, RemoteDMATransfer
+from concourse.mybir import AluOpType, AxisListType, ActivationFunctionType
+
+N = 4
+B = 128
+W = 2 * B
+NE = 2
+N_FAR = 4
+N_NEAR = 4
+SPLIT_CALLS = False
+NT = 8 - 2 * NE
+
+SCRATCH = {
+    "kv": ("sbuf", [128, N * W], "bfloat16"),
+    "qs": ("sbuf", [128, B], "bfloat16"),
+    "ident": ("sbuf", [128, B], "bfloat16"),
+    "p": ("sbuf", [128, N * B], "bfloat16"),
+    "pt": ("sbuf", [128, N * B], "bfloat16"),
+    "negm": ("sbuf", [128, 4], "float32"),
+    "aa": ("sbuf", [128, 4], "float32"),
+    "lac": ("sbuf", [128, 4 * NE], "float32"),
+    "ll": ("sbuf", [128, 4], "float32"),
+    "rl": ("sbuf", [128, 4], "float32"),
+    "dg": ("sbuf", [128, (NE - 1) * B], "bfloat16"),
+    "oe": ("sbuf", [128, (NE - 1) * B], "bfloat16"),
+    "ysb": ("sbuf", [128, B], "bfloat16"),
+}
+for _e in range(NE):
+    SCRATCH["s%d" % _e] = ("psum", [128, 512], "float32")
+    SCRATCH["o%d" % _e] = ("psum", [128, 512], "float32")
+for _i in range(NT):
+    SCRATCH["t%d" % _i] = ("psum", [128, 1024], "bfloat16")
+
+SEMAPHORES = ["ldkv", "ldq", "cone", "cid", "sent", "rls", "yd", "st"]
+SEMAPHORES += ["arr%d" % _j for _j in range(N)]
+SEMAPHORES += ["%s%d" % (_n, _e) for _n in ("sc", "mx", "mp", "ae", "dg", "ca", "ls", "pv", "oe") for _e in range(NE)]
+SEMAPHORES += ["%s%d" % (_n, _i) for _n in ("ex", "tp", "cp") for _i in range(N)]
+
+
+def _take(allowed, used, n):
+    m = 0
+    for b in range(allowed.bit_length()):
+        if n and (allowed >> b) & 1 and not (used >> b) & 1:
+            m |= 1 << b
+            n -= 1
+    return m
+
+
+def rank_program(g, core, T, topo):
+    r = T.rank_of(core)
+    if r is None:
+        return
+    sem, cores = T.sem, T.cores
+    PE, V, A, SY = g.tensor, g.vector, g.scalar, g.sync
+    Exp = ActivationFunctionType.Exp
+    mult = AluOpType.mult
+
+    def on_chip(a, b):
+        return topo.host(a) == topo.host(b) and topo.chip(a) == topo.chip(b)
+
+    def n_eng(a, b):
+        return N_NEAR if on_chip(a, b) else N_FAR
+
+    near = [j for j in range(N) if j != r and on_chip(cores[j], core)]
+    far = [j for j in range(N) if j != r and not on_chip(cores[j], core)]
+    far.sort(key=lambda j: topo.die(cores[j]) != topo.die(core))
+    if NE == 2:
+        steps = [[r], near + far]
+    else:
+        steps = [[r], near, far]
+
+    def kcol(j):
+        return T.kv[:, j * W:j * W + B]
+
+    def vcol(j):
+        return T.kv[:, j * W + B:(j + 1) * W]
+
+    def blk(t, i):
+        return t[:, i * B:(i + 1) * B]
+
+    def col(t, c):
+        return t[:, c:c + 1]
+
+    SY.dma_start(kcol(r), T.k[:]).then_inc(sem.ldkv, 16)
+    A.dma_start(vcol(r), T.v[:]).then_inc(sem.ldkv, 16)
+    SY.dma_start(T.qs[:], T.q[:]).then_inc(sem.ldq, 16)
+
+    V.memset(T.ident[:], 1.0).then_inc(sem.cone, 1)
+    g.wait_ge(sem.cone, 1)
+    g.affine_select(T.ident[:], T.ident[:], [[-1, B]], AluOpType.is_equal, 0.0, 0, 1).then_inc(sem.cid, 1)
+
+    slot = T.kv[:, r * W:(r + 1) * W]
+    used, total = 0, 0
+    calls = [far, near] if SPLIT_CALLS else [far + near]
+    g.wait_ge(sem.ldkv, 32)
+    for dests in calls:
+        trs = []
+        for j in dests:
+            m = _take(topo.mask(core, cores[j]), used, n_eng(core, cores[j]))
+            used |= m
+            total += n_eng(core, cores[j])
+            rid, pid = topo.addr(cores[j], core)
+            trs.append(RemoteDMATransfer(dst_ids=[DstId(rid=rid, pnc=pid)], dma_engine_mask=m,
+                                         remote_sem=sem["arr%d" % r], src=slot, dst=slot))
+        g.remote_dma_fused(trs, local_sem=sem.sent)
+    g.wait_ge(sem.sent, total)
+
+    V.wait_ge(sem.cid, 1)
+    PE.wait_ge(sem.cid, 1)
+    PE.wait_ge(sem.ldq, 16)
+    PE.wait_ge(sem.ldkv, 32)
+    i0 = 0
+    for e, blocks in enumerate(steps):
+        nb = len(blocks)
+        last = e == NE - 1
+        Sb, Ob = T["s%d" % e], T["o%d" % e][:, 0:B]
+        nm = col(T.negm, e)
+
+        if e:
+            PE.wait_ge(sem["mp%d" % e], 1)
+        for c, j in enumerate(blocks):
+            if j != r:
+                PE.wait_ge(sem["arr%d" % j], n_eng(cores[j], core))
+            PE.matmul(blk(Sb, c), T.qs[:], kcol(j), True, True).then_inc(sem["sc%d" % e], 1)
+
+        V.wait_ge(sem["sc%d" % e], nb)
+        V.tensor_reduce(nm, Sb[:, 0:nb * B + (1 if e else 0)], AxisListType.X, AluOpType.max,
+                        negate=True).then_inc(sem["mx%d" % e], 1)
+        if not last:
+            wn = len(steps[e + 1]) * B
+            V.wait_ge(sem["mx%d" % e], 1)
+            V.tensor_scalar(col(T["s%d" % (e + 1)], wn), nm, -1.0, None, mult).then_inc(sem["mp%d" % (e + 1)], 1)
+
+        A.wait_ge(sem["mx%d" % e], 1)
+        if e:
+            A.activation(col(T.aa, e), col(T.negm, e - 1), Exp, bias=nm, scale=-1.0).then_inc(sem["ae%d" % e], 1)
+        for c in range(nb):
+            A.activation(blk(T.p, i0 + c), blk(Sb, c), Exp, bias=nm, scale=1.0,
+                         accum_out=col(T.lac, 4 * e + 1 + c)).then_inc(sem["ex%d" % (i0 + c)], 1)
+        if e:
+            V.wait_ge(sem["ae%d" % e], 1)
+            V.tensor_scalar(blk(T.dg, e - 1), T.ident[:], col(T.aa, e), None, mult).then_inc(sem["dg%d" % e], 1)
+            V.tensor_tensor(col(T.lac, 4 * e), col(T.ll, e - 1), col(T.aa, e), mult).then_inc(sem["ca%d" % e], 1)
+
+        for c in range(nb):
+            i = i0 + c
+            PE.wait_ge(sem["ex%d" % i], 1)
+            if i >= NT:
+                PE.wait_ge(sem["cp%d" % (i - NT)], 1)
+            PE.transpose(T["t%d" % (i % NT)][:, 0:B], blk(T.p, i), T.ident[:]).then_inc(sem["tp%d" % i], 1)
+            V.wait_ge(sem["tp%d" % i], 1)
+            V.tensor_copy(blk(T.pt, i), T["t%d" % (i % NT)][:, 0:B]).then_inc(sem["cp%d" % i], 1)
+
+        if e:
+            PE.wait_ge(sem["dg%d" % e], 1)
+            PE.wait_ge(sem["oe%d" % (e - 1)], 1)
+            PE.matmul(Ob, blk(T.dg, e - 1), blk(T.oe, e - 1), True, False)
+        for c, j in enumerate(blocks):
+            PE.wait_ge(sem["cp%d" % (i0 + c)], 1)
+            mm = PE.matmul(Ob, blk(T.pt, i0 + c), vcol(j), c == 0 and e == 0, c == nb - 1)
+            if c == nb - 1:
+                mm.then_inc(sem["pv%d" % e], 1)
+
+        for c in range(nb):
+            V.wait_ge(sem["ex%d" % (i0 + c)], 1)
+        if e:
+            V.wait_ge(sem["ca%d" % e], 1)
+        V.tensor_reduce(col(T.ll, e), T.lac[:, 4 * e + (0 if e else 1):4 * e + 1 + nb], AxisListType.X,
+                        AluOpType.add).then_inc(sem["ls%d" % e], 1)
+        V.wait_ge(sem["ls%d" % e], 1)
+        if last:
+            V.reciprocal(col(T.rl, 0), col(T.ll, e)).then_inc(sem.rls, 1)
+            V.wait_ge(sem.rls, 1)
+            V.wait_ge(sem["pv%d" % e], 1)
+            V.tensor_scalar(T.ysb[:], Ob, col(T.rl, 0), None, mult).then_inc(sem.yd, 1)
+        else:
+            V.wait_ge(sem["pv%d" % e], 1)
+            V.tensor_copy(blk(T.oe, e), Ob).then_inc(sem["oe%d" % e], 1)
+        i0 += nb
+
+    SY.wait_ge(sem.yd, 1)
+    SY.dma_start(T.y[:], T.ysb[:]).then_inc(sem.st, 16)
+    SY.wait_ge(sem.st, 16)

@@ -4,11 +4,8 @@ from concourse.mybir import AluOpType, AxisListType, ActivationFunctionType
 N = 4
 B = 128
 W = 2 * B
-NE = 2
 N_FAR = 4
 N_NEAR = 4
-SPLIT_CALLS = False
-NT = 8 - 2 * NE
 
 SCRATCH = {
     "kv": ("sbuf", [128, N * W], "bfloat16"),
@@ -18,23 +15,22 @@ SCRATCH = {
     "pt": ("sbuf", [128, N * B], "bfloat16"),
     "negm": ("sbuf", [128, 4], "float32"),
     "aa": ("sbuf", [128, 4], "float32"),
-    "lac": ("sbuf", [128, 4 * NE], "float32"),
-    "ll": ("sbuf", [128, 4], "float32"),
+    "lac": ("sbuf", [128, 8], "float32"),
     "rl": ("sbuf", [128, 4], "float32"),
-    "dg": ("sbuf", [128, (NE - 1) * B], "bfloat16"),
-    "oe": ("sbuf", [128, (NE - 1) * B], "bfloat16"),
+    "dg": ("sbuf", [128, B], "bfloat16"),
+    "oe": ("sbuf", [128, B], "bfloat16"),
     "ysb": ("sbuf", [128, B], "bfloat16"),
+    "s0": ("psum", [128, 512], "float32"),
+    "s1": ("psum", [128, 512], "float32"),
+    "o0": ("psum", [128, 512], "float32"),
+    "o1": ("psum", [128, 512], "float32"),
 }
-for _e in range(NE):
-    SCRATCH["s%d" % _e] = ("psum", [128, 512], "float32")
-    SCRATCH["o%d" % _e] = ("psum", [128, 512], "float32")
-for _i in range(NT):
+for _i in range(N):
     SCRATCH["t%d" % _i] = ("psum", [128, 1024], "bfloat16")
 
-SEMAPHORES = ["ldkv", "ldq", "cone", "cid", "sent", "rls", "yd", "st"]
-SEMAPHORES += ["arr%d" % _j for _j in range(N)]
-SEMAPHORES += ["%s%d" % (_n, _e) for _n in ("sc", "mx", "mp", "ae", "dg", "ca", "ls", "pv", "oe") for _e in range(NE)]
-SEMAPHORES += ["%s%d" % (_n, _i) for _n in ("ex", "tp", "cp") for _i in range(N)]
+SEMAPHORES = ["ldk", "ldv", "ldq", "cone", "cid", "sent", "sc0", "sc1", "mx0", "mx1", "mp", "ae", "dgs", "ca", "ls",
+              "pv0", "pv1", "oes", "rls", "yd", "st"]
+SEMAPHORES += ["%s%d" % (_n, _j) for _n in ("ak", "av", "ex", "tp", "cp") for _j in range(N)]
 
 
 def _take(allowed, used, n):
@@ -53,6 +49,7 @@ def rank_program(g, core, T, topo):
     sem, cores = T.sem, T.cores
     PE, V, A, SY = g.tensor, g.vector, g.scalar, g.sync
     Exp = ActivationFunctionType.Exp
+    X = AxisListType.X
     mult = AluOpType.mult
 
     def on_chip(a, b):
@@ -64,10 +61,7 @@ def rank_program(g, core, T, topo):
     near = [j for j in range(N) if j != r and on_chip(cores[j], core)]
     far = [j for j in range(N) if j != r and not on_chip(cores[j], core)]
     far.sort(key=lambda j: topo.die(cores[j]) != topo.die(core))
-    if NE == 2:
-        steps = [[r], near + far]
-    else:
-        steps = [[r], near, far]
+    others = near + far
 
     def kcol(j):
         return T.kv[:, j * W:j * W + B]
@@ -81,102 +75,102 @@ def rank_program(g, core, T, topo):
     def col(t, c):
         return t[:, c:c + 1]
 
-    SY.dma_start(kcol(r), T.k[:]).then_inc(sem.ldkv, 16)
-    A.dma_start(vcol(r), T.v[:]).then_inc(sem.ldkv, 16)
+    def tbank(i):
+        return T["t%d" % i][:, 0:B]
+
+    S0, O0, O1 = T.s0[:, 0:B], T.o0[:, 0:B], T.o1[:, 0:B]
+    nm0, nm1 = col(T.negm, 0), col(T.negm, 1)
+    NB = len(others)
+
+    SY.dma_start(kcol(r), T.k[:]).then_inc(sem.ldk, 16)
     SY.dma_start(T.qs[:], T.q[:]).then_inc(sem.ldq, 16)
+    A.wait_ge(sem.ldk, 16)
+    A.dma_start(vcol(r), T.v[:]).then_inc(sem.ldv, 16)
 
     V.memset(T.ident[:], 1.0).then_inc(sem.cone, 1)
     g.wait_ge(sem.cone, 1)
     g.affine_select(T.ident[:], T.ident[:], [[-1, B]], AluOpType.is_equal, 0.0, 0, 1).then_inc(sem.cid, 1)
 
-    slot = T.kv[:, r * W:(r + 1) * W]
-    used, total = 0, 0
-    calls = [far, near] if SPLIT_CALLS else [far + near]
-    g.wait_ge(sem.ldkv, 32)
-    for dests in calls:
+    masks, used, total = {}, 0, 0
+    for j in far + near:
+        masks[j] = _take(topo.mask(core, cores[j]), used, n_eng(core, cores[j]))
+        used |= masks[j]
+    for loaded, part, name in ((sem.ldk, kcol(r), "ak%d"), (sem.ldv, vcol(r), "av%d")):
         trs = []
-        for j in dests:
-            m = _take(topo.mask(core, cores[j]), used, n_eng(core, cores[j]))
-            used |= m
+        for j in far + near:
             total += n_eng(core, cores[j])
             rid, pid = topo.addr(cores[j], core)
-            trs.append(RemoteDMATransfer(dst_ids=[DstId(rid=rid, pnc=pid)], dma_engine_mask=m,
-                                         remote_sem=sem["arr%d" % r], src=slot, dst=slot))
+            trs.append(RemoteDMATransfer(dst_ids=[DstId(rid=rid, pnc=pid)], dma_engine_mask=masks[j],
+                                         remote_sem=sem[name % r], src=part, dst=part))
+        g.wait_ge(loaded, 16)
         g.remote_dma_fused(trs, local_sem=sem.sent)
     g.wait_ge(sem.sent, total)
 
-    V.wait_ge(sem.cid, 1)
-    PE.wait_ge(sem.cid, 1)
     PE.wait_ge(sem.ldq, 16)
-    PE.wait_ge(sem.ldkv, 32)
-    i0 = 0
-    for e, blocks in enumerate(steps):
-        nb = len(blocks)
-        last = e == NE - 1
-        Sb, Ob = T["s%d" % e], T["o%d" % e][:, 0:B]
-        nm = col(T.negm, e)
+    PE.wait_ge(sem.ldk, 16)
+    PE.matmul(S0, T.qs[:], kcol(r), True, True).then_inc(sem.sc0, 1)
+    V.wait_ge(sem.sc0, 1)
+    V.tensor_reduce(nm0, S0, X, AluOpType.max, negate=True).then_inc(sem.mx0, 1)
+    V.wait_ge(sem.mx0, 1)
+    V.tensor_scalar(col(T.s1, NB * B), nm0, -1.0, None, mult).then_inc(sem.mp, 1)
+    A.wait_ge(sem.mx0, 1)
+    A.activation(blk(T.p, 0), S0, Exp, bias=nm0, scale=1.0, accum_out=col(T.lac, 4)).then_inc(sem.ex0, 1)
 
-        if e:
-            PE.wait_ge(sem["mp%d" % e], 1)
-        for c, j in enumerate(blocks):
-            if j != r:
-                PE.wait_ge(sem["arr%d" % j], n_eng(cores[j], core))
-            PE.matmul(blk(Sb, c), T.qs[:], kcol(j), True, True).then_inc(sem["sc%d" % e], 1)
+    PE.wait_ge(sem.mp, 1)
+    for c, j in enumerate(others):
+        PE.wait_ge(sem["ak%d" % j], n_eng(cores[j], core))
+        PE.matmul(blk(T.s1, c), T.qs[:], kcol(j), True, True).then_inc(sem.sc1, 1)
+    V.wait_ge(sem.sc1, NB)
+    V.tensor_reduce(nm1, T.s1[:, 0:NB * B + 1], X, AluOpType.max, negate=True).then_inc(sem.mx1, 1)
+    A.wait_ge(sem.mx1, 1)
+    A.activation(col(T.aa, 0), nm0, Exp, bias=nm1, scale=-1.0).then_inc(sem.ae, 1)
+    for i in range(1, N):
+        A.activation(blk(T.p, i), blk(T.s1, i - 1), Exp, bias=nm1, scale=1.0,
+                     accum_out=col(T.lac, i)).then_inc(sem["ex%d" % i], 1)
 
-        V.wait_ge(sem["sc%d" % e], nb)
-        V.tensor_reduce(nm, Sb[:, 0:nb * B + (1 if e else 0)], AxisListType.X, AluOpType.max,
-                        negate=True).then_inc(sem["mx%d" % e], 1)
-        if not last:
-            wn = len(steps[e + 1]) * B
-            V.wait_ge(sem["mx%d" % e], 1)
-            V.tensor_scalar(col(T["s%d" % (e + 1)], wn), nm, -1.0, None, mult).then_inc(sem["mp%d" % (e + 1)], 1)
+    PE.wait_ge(sem.cid, 1)
+    PE.wait_ge(sem.ex0, 1)
+    PE.transpose(tbank(0), blk(T.p, 0), T.ident[:]).then_inc(sem.tp0, 1)
+    V.wait_ge(sem.tp0, 1)
+    V.tensor_copy(blk(T.pt, 0), tbank(0)).then_inc(sem.cp0, 1)
+    PE.wait_ge(sem.cp0, 1)
+    PE.wait_ge(sem.ldv, 16)
+    PE.matmul(O0, blk(T.pt, 0), vcol(r), True, True).then_inc(sem.pv0, 1)
+    V.wait_ge(sem.pv0, 1)
+    V.tensor_copy(T.oe[:], O0).then_inc(sem.oes, 1)
 
-        A.wait_ge(sem["mx%d" % e], 1)
-        if e:
-            A.activation(col(T.aa, e), col(T.negm, e - 1), Exp, bias=nm, scale=-1.0).then_inc(sem["ae%d" % e], 1)
-        for c in range(nb):
-            A.activation(blk(T.p, i0 + c), blk(Sb, c), Exp, bias=nm, scale=1.0,
-                         accum_out=col(T.lac, 4 * e + 1 + c)).then_inc(sem["ex%d" % (i0 + c)], 1)
-        if e:
-            V.wait_ge(sem["ae%d" % e], 1)
-            V.tensor_scalar(blk(T.dg, e - 1), T.ident[:], col(T.aa, e), None, mult).then_inc(sem["dg%d" % e], 1)
-            V.tensor_tensor(col(T.lac, 4 * e), col(T.ll, e - 1), col(T.aa, e), mult).then_inc(sem["ca%d" % e], 1)
+    V.wait_ge(sem.cid, 1)
+    V.wait_ge(sem.ae, 1)
+    V.tensor_scalar(T.dg[:], T.ident[:], col(T.aa, 0), None, mult).then_inc(sem.dgs, 1)
+    V.wait_ge(sem.ex0, 1)
+    V.tensor_tensor(col(T.lac, 0), col(T.lac, 4), col(T.aa, 0), mult).then_inc(sem.ca, 1)
 
-        for c in range(nb):
-            i = i0 + c
-            PE.wait_ge(sem["ex%d" % i], 1)
-            if i >= NT:
-                PE.wait_ge(sem["cp%d" % (i - NT)], 1)
-            PE.transpose(T["t%d" % (i % NT)][:, 0:B], blk(T.p, i), T.ident[:]).then_inc(sem["tp%d" % i], 1)
-            V.wait_ge(sem["tp%d" % i], 1)
-            V.tensor_copy(blk(T.pt, i), T["t%d" % (i % NT)][:, 0:B]).then_inc(sem["cp%d" % i], 1)
+    for i in range(1, N):
+        PE.wait_ge(sem["ex%d" % i], 1)
+        PE.transpose(tbank(i), blk(T.p, i), T.ident[:]).then_inc(sem["tp%d" % i], 1)
+        V.wait_ge(sem["tp%d" % i], 1)
+        V.tensor_copy(blk(T.pt, i), tbank(i)).then_inc(sem["cp%d" % i], 1)
 
-        if e:
-            PE.wait_ge(sem["dg%d" % e], 1)
-            PE.wait_ge(sem["oe%d" % (e - 1)], 1)
-            PE.matmul(Ob, blk(T.dg, e - 1), blk(T.oe, e - 1), True, False)
-        for c, j in enumerate(blocks):
-            PE.wait_ge(sem["cp%d" % (i0 + c)], 1)
-            mm = PE.matmul(Ob, blk(T.pt, i0 + c), vcol(j), c == 0 and e == 0, c == nb - 1)
-            if c == nb - 1:
-                mm.then_inc(sem["pv%d" % e], 1)
+    for c, j in enumerate(others):
+        if c == NB - 1:
+            PE.wait_ge(sem.dgs, 1)
+            PE.wait_ge(sem.oes, 1)
+            PE.matmul(O1, T.dg[:], T.oe[:], False, False)
+        PE.wait_ge(sem["cp%d" % (1 + c)], 1)
+        PE.wait_ge(sem["av%d" % j], n_eng(cores[j], core))
+        mm = PE.matmul(O1, blk(T.pt, 1 + c), vcol(j), c == 0, c == NB - 1)
+        if c == NB - 1:
+            mm.then_inc(sem.pv1, 1)
 
-        for c in range(nb):
-            V.wait_ge(sem["ex%d" % (i0 + c)], 1)
-        if e:
-            V.wait_ge(sem["ca%d" % e], 1)
-        V.tensor_reduce(col(T.ll, e), T.lac[:, 4 * e + (0 if e else 1):4 * e + 1 + nb], AxisListType.X,
-                        AluOpType.add).then_inc(sem["ls%d" % e], 1)
-        V.wait_ge(sem["ls%d" % e], 1)
-        if last:
-            V.reciprocal(col(T.rl, 0), col(T.ll, e)).then_inc(sem.rls, 1)
-            V.wait_ge(sem.rls, 1)
-            V.wait_ge(sem["pv%d" % e], 1)
-            V.tensor_scalar(T.ysb[:], Ob, col(T.rl, 0), None, mult).then_inc(sem.yd, 1)
-        else:
-            V.wait_ge(sem["pv%d" % e], 1)
-            V.tensor_copy(blk(T.oe, e), Ob).then_inc(sem["oe%d" % e], 1)
-        i0 += nb
+    for i in range(1, N):
+        V.wait_ge(sem["ex%d" % i], 1)
+    V.wait_ge(sem.ca, 1)
+    V.tensor_reduce(col(T.lac, 5), T.lac[:, 0:N], X, AluOpType.add).then_inc(sem.ls, 1)
+    V.wait_ge(sem.ls, 1)
+    V.reciprocal(col(T.rl, 0), col(T.lac, 5)).then_inc(sem.rls, 1)
+    V.wait_ge(sem.rls, 1)
+    V.wait_ge(sem.pv1, 1)
+    V.tensor_scalar(T.ysb[:], O1, col(T.rl, 0), None, mult).then_inc(sem.yd, 1)
 
     SY.wait_ge(sem.yd, 1)
     SY.dma_start(T.y[:], T.ysb[:]).then_inc(sem.st, 16)

from concourse.bass import DstId, RemoteDMATransfer
from concourse.mybir import AluOpType, AxisListType, ActivationFunctionType

N = 4
B = 128
W = 2 * B
N_FAR = 4
N_NEAR = 4

SCRATCH = {
    "kv": ("sbuf", [128, N * W], "bfloat16"),
    "qs": ("sbuf", [128, B], "bfloat16"),
    "ident": ("sbuf", [128, B], "bfloat16"),
    "p": ("sbuf", [128, N * B], "bfloat16"),
    "pt": ("sbuf", [128, N * B], "bfloat16"),
    "negm": ("sbuf", [128, 4], "float32"),
    "aa": ("sbuf", [128, 4], "float32"),
    "lac": ("sbuf", [128, 8], "float32"),
    "rl": ("sbuf", [128, 4], "float32"),
    "dg": ("sbuf", [128, B], "bfloat16"),
    "oe": ("sbuf", [128, B], "bfloat16"),
    "ysb": ("sbuf", [128, B], "bfloat16"),
    "s0": ("psum", [128, 512], "float32"),
    "s1": ("psum", [128, 512], "float32"),
    "o0": ("psum", [128, 512], "float32"),
    "o1": ("psum", [128, 512], "float32"),
}
for _i in range(N):
    SCRATCH["t%d" % _i] = ("psum", [128, 1024], "bfloat16")

SEMAPHORES = ["ldk", "ldv", "ldq", "cone", "cid", "sent", "sc0", "sc1", "mx0", "mx1", "mp", "ae", "dgs", "ca", "ls",
              "pv0", "pv1", "oes", "rls", "yd", "st"]
SEMAPHORES += ["%s%d" % (_n, _j) for _n in ("ak", "av", "ex", "tp", "cp") for _j in range(N)]


def _take(allowed, used, n):
    m = 0
    for b in range(allowed.bit_length()):
        if n and (allowed >> b) & 1 and not (used >> b) & 1:
            m |= 1 << b
            n -= 1
    return m


def rank_program(g, core, T, topo):
    r = T.rank_of(core)
    if r is None:
        return
    sem, cores = T.sem, T.cores
    PE, V, A, SY = g.tensor, g.vector, g.scalar, g.sync
    Exp = ActivationFunctionType.Exp
    X = AxisListType.X
    mult = AluOpType.mult

    def on_chip(a, b):
        return topo.host(a) == topo.host(b) and topo.chip(a) == topo.chip(b)

    def n_eng(a, b):
        return N_NEAR if on_chip(a, b) else N_FAR

    near = [j for j in range(N) if j != r and on_chip(cores[j], core)]
    far = [j for j in range(N) if j != r and not on_chip(cores[j], core)]
    far.sort(key=lambda j: topo.die(cores[j]) != topo.die(core))
    others = near + far

    def kcol(j):
        return T.kv[:, j * W:j * W + B]

    def vcol(j):
        return T.kv[:, j * W + B:(j + 1) * W]

    def blk(t, i):
        return t[:, i * B:(i + 1) * B]

    def col(t, c):
        return t[:, c:c + 1]

    def tbank(i):
        return T["t%d" % i][:, 0:B]

    S0, O0, O1 = T.s0[:, 0:B], T.o0[:, 0:B], T.o1[:, 0:B]
    nm0, nm1 = col(T.negm, 0), col(T.negm, 1)
    NB = len(others)

    SY.dma_start(kcol(r), T.k[:]).then_inc(sem.ldk, 16)
    SY.dma_start(T.qs[:], T.q[:]).then_inc(sem.ldq, 16)
    A.wait_ge(sem.ldk, 16)
    A.dma_start(vcol(r), T.v[:]).then_inc(sem.ldv, 16)

    V.memset(T.ident[:], 1.0).then_inc(sem.cone, 1)
    g.wait_ge(sem.cone, 1)
    g.affine_select(T.ident[:], T.ident[:], [[-1, B]], AluOpType.is_equal, 0.0, 0, 1).then_inc(sem.cid, 1)

    masks, used, total = {}, 0, 0
    for j in far + near:
        masks[j] = _take(topo.mask(core, cores[j]), used, n_eng(core, cores[j]))
        used |= masks[j]
    for loaded, part, name in ((sem.ldk, kcol(r), "ak%d"), (sem.ldv, vcol(r), "av%d")):
        trs = []
        for j in far + near:
            total += n_eng(core, cores[j])
            rid, pid = topo.addr(cores[j], core)
            trs.append(RemoteDMATransfer(dst_ids=[DstId(rid=rid, pnc=pid)], dma_engine_mask=masks[j],
                                         remote_sem=sem[name % r], src=part, dst=part))
        g.wait_ge(loaded, 16)
        g.remote_dma_fused(trs, local_sem=sem.sent)
    g.wait_ge(sem.sent, total)

    PE.wait_ge(sem.ldq, 16)
    PE.wait_ge(sem.ldk, 16)
    PE.matmul(S0, T.qs[:], kcol(r), True, True).then_inc(sem.sc0, 1)
    V.wait_ge(sem.sc0, 1)
    V.tensor_reduce(nm0, S0, X, AluOpType.max, negate=True).then_inc(sem.mx0, 1)
    V.wait_ge(sem.mx0, 1)
    V.tensor_scalar(col(T.s1, NB * B), nm0, -1.0, None, mult).then_inc(sem.mp, 1)
    A.wait_ge(sem.mx0, 1)
    A.activation(blk(T.p, 0), S0, Exp, bias=nm0, scale=1.0, accum_out=col(T.lac, 4)).then_inc(sem.ex0, 1)

    PE.wait_ge(sem.mp, 1)
    for c, j in enumerate(others):
        PE.wait_ge(sem["ak%d" % j], n_eng(cores[j], core))
        PE.matmul(blk(T.s1, c), T.qs[:], kcol(j), True, True).then_inc(sem.sc1, 1)
    V.wait_ge(sem.sc1, NB)
    V.tensor_reduce(nm1, T.s1[:, 0:NB * B + 1], X, AluOpType.max, negate=True).then_inc(sem.mx1, 1)
    A.wait_ge(sem.mx1, 1)
    A.activation(col(T.aa, 0), nm0, Exp, bias=nm1, scale=-1.0).then_inc(sem.ae, 1)
    for i in range(1, N):
        A.activation(blk(T.p, i), blk(T.s1, i - 1), Exp, bias=nm1, scale=1.0,
                     accum_out=col(T.lac, i)).then_inc(sem["ex%d" % i], 1)

    PE.wait_ge(sem.cid, 1)
    PE.wait_ge(sem.ex0, 1)
    PE.transpose(tbank(0), blk(T.p, 0), T.ident[:]).then_inc(sem.tp0, 1)
    V.wait_ge(sem.tp0, 1)
    V.tensor_copy(blk(T.pt, 0), tbank(0)).then_inc(sem.cp0, 1)
    PE.wait_ge(sem.cp0, 1)
    PE.wait_ge(sem.ldv, 16)
    PE.matmul(O0, blk(T.pt, 0), vcol(r), True, True).then_inc(sem.pv0, 1)
    V.wait_ge(sem.pv0, 1)
    V.tensor_copy(T.oe[:], O0).then_inc(sem.oes, 1)

    V.wait_ge(sem.cid, 1)
    V.wait_ge(sem.ae, 1)
    V.tensor_scalar(T.dg[:], T.ident[:], col(T.aa, 0), None, mult).then_inc(sem.dgs, 1)
    V.wait_ge(sem.ex0, 1)
    V.tensor_tensor(col(T.lac, 0), col(T.lac, 4), col(T.aa, 0), mult).then_inc(sem.ca, 1)

    for i in range(1, N):
        PE.wait_ge(sem["ex%d" % i], 1)
        PE.transpose(tbank(i), blk(T.p, i), T.ident[:]).then_inc(sem["tp%d" % i], 1)
        V.wait_ge(sem["tp%d" % i], 1)
        V.tensor_copy(blk(T.pt, i), tbank(i)).then_inc(sem["cp%d" % i], 1)

    for c, j in enumerate(others):
        if c == NB - 1:
            PE.wait_ge(sem.dgs, 1)
            PE.wait_ge(sem.oes, 1)
            PE.matmul(O1, T.dg[:], T.oe[:], False, False)
        PE.wait_ge(sem["cp%d" % (1 + c)], 1)
        PE.wait_ge(sem["av%d" % j], n_eng(cores[j], core))
        mm = PE.matmul(O1, blk(T.pt, 1 + c), vcol(j), c == 0, c == NB - 1)
        if c == NB - 1:
            mm.then_inc(sem.pv1, 1)

    for i in range(1, N):
        V.wait_ge(sem["ex%d" % i], 1)
    V.wait_ge(sem.ca, 1)
    V.tensor_reduce(col(T.lac, 5), T.lac[:, 0:N], X, AluOpType.add).then_inc(sem.ls, 1)
    V.wait_ge(sem.ls, 1)
    V.reciprocal(col(T.rl, 0), col(T.lac, 5)).then_inc(sem.rls, 1)
    V.wait_ge(sem.rls, 1)
    V.wait_ge(sem.pv1, 1)
    V.tensor_scalar(T.ysb[:], O1, col(T.rl, 0), None, mult).then_inc(sem.yd, 1)

    SY.wait_ge(sem.yd, 1)
    SY.dma_start(T.y[:], T.ysb[:]).then_inc(sem.st, 16)
    SY.wait_ge(sem.st, 16)
